import numpy as np
import ml_dtypes


def mxq(x, axis, fmt="e4m3"):
    dtype, down = {"e4m3": (ml_dtypes.float8_e4m3fn, 7), "e5m2": (ml_dtypes.float8_e5m2, 14)}[fmt]
    v = np.moveaxis(np.asarray(x, np.float32).astype(ml_dtypes.bfloat16).astype(np.float64), axis, -1)
    blocks = v.reshape(v.shape[:-1] + (-1, 32))
    amax = np.abs(blocks).max(-1, keepdims=True)
    byte = np.maximum(np.where(amax > 0, np.frexp(amax)[1] - 1 + 127, 0) - down, 1)
    scale = np.exp2(byte - 127.0)
    codes = (blocks / scale).astype(np.float32).astype(dtype).astype(np.float64)
    return np.moveaxis((codes * scale).reshape(v.shape), -1, axis)


WIDE = False


def mx_kscale(k, group=512):
    if not WIDE:
        return np.ones(k)
    levels = np.array([10, -10, 5, -5, 0])
    if group != 512:
        return np.exp2(np.random.permutation(np.resize(levels, k // group))).repeat(group)
    if k % 512:
        return np.exp2(np.random.permutation(np.resize(levels, k // 32))).repeat(32)
    a = np.empty((k // 512, 16))
    for p in range(k // 512):
        a[p, :8] = np.random.permutation(np.resize(levels, 8))
        for g in range(8):
            far = levels[np.abs(levels - a[p, g]) >= 10]
            a[p, g + 8] = far[np.random.randint(len(far))]
    return np.exp2(a.ravel()).repeat(32)


def f64(x):
    return np.asarray(x).astype(np.float64)


def striped(idx):
    return np.tile(np.asarray(idx).reshape(-1, 16).T, (8, 1)).astype(np.uint16)


def unstriped(offs):
    return offs[:16].T.reshape(-1).astype(np.int64)


H, KV, D, NQ, N = 4, 2, 256, 512, 512
CAP = 2.0


def setup_inputs():
    n = np.random.standard_normal
    s = mx_kscale(D, 0)[:, None]
    u = mx_kscale(N)
    t = np.random.uniform(0.5, 2.0, N) * u
    v = n((KV, N, 128))
    return {
        "qT": (n((H, D, NQ)) * s * (0.70 / np.sqrt(D))).astype(np.float32),
        "kT": (n((KV, D, N)) / s).astype(np.float32),
        "t": t.reshape(N, 1).astype(np.float32),
        "v": (v / t[:, None]).astype(np.float32),
        "gn": np.tile(np.random.uniform(0.5, 2.0, 128), (128, 1)).astype(np.float32),
    }


def reference(qT, kT, t, v, gn):
    a = np.repeat(mxq(f64(kT), 1, "e4m3"), H // KV, 0).transpose(0, 2, 1) @ mxq(f64(qT), 1, "e4m3")
    a = CAP * np.tanh(a / CAP)
    p = a / (1.0 + np.exp(-a))
    w = p * f64(t)
    y = mxq(w, 1, "e4m3").transpose(0, 2, 1) @ np.repeat(mxq(f64(v), 1, "e4m3"), H // KV, 0)
    y = y / 16.0
    y = y / np.sqrt(np.mean(np.square(y), -1, keepdims=True) + 1e-5) * f64(gn)[:1]
    return y

@@ -1,0 +1,256 @@
+from contextlib import ExitStack
+
+import concourse.mybir as mybir
+
+H, KV, D, NQ, N, E = 4, 2, 256, 512, 512, 128
+FLOPS = 2 * H * N * NQ * D + 2 * H * NQ * N * E
+
+F32 = mybir.dt.float32
+BF16 = mybir.dt.bfloat16
+U32 = mybir.dt.uint32
+U8 = mybir.dt.uint8
+FP8X4 = mybir.dt.float8_e4m3fn_x4
+ACT = mybir.ActivationFunctionType
+ALU = mybir.AluOpType
+
+P = 128
+ROWS = 64
+PACK = 4
+QT = 128
+TILES = NQ // QT
+UNITS = H * TILES
+HALF = N // 2
+EPS = 1e-5 * 256.0
+HEAD_SETS = ((1, 2), (0, 3))
+K_SPLIT = 40
+
+
+def tile_rows_a_silu_cap_onorm_kernel(tc, qT, kT, t, v, gn, out):
+    nc = tc.nc
+    with ExitStack() as ctx:
+        keep = ctx.enter_context(tc.tile_pool(name="keep", bufs=1))
+        work = ctx.enter_context(tc.tile_pool(name="work", bufs=4))
+        psum = ctx.enter_context(tc.psum_pool(name="psum", bufs=1))
+        ctx.enter_context(tc.manual_schedule())
+
+        k_raw = [keep.tile([P, PACK, HALF], F32, name="k_raw%d" % c) for c in range(2)]
+        q_raw = [keep.tile([P, PACK, NQ], F32, name="q_raw%d" % a) for a in range(2)]
+        v_raw = keep.tile([P, KV, PACK, E], F32)
+        t_sb = keep.tile([P, PACK], F32)
+        gn_sb = keep.tile([P, E], F32)
+        k_bf = keep.tile([P, PACK, P, PACK], BF16, align_bytes=64)
+        q_bf = keep.tile([P, 2, NQ, PACK], BF16, align_bytes=64)
+        v_bf = keep.tile([P, KV, E, PACK], BF16, align_bytes=64)
+        k_codes = keep.tile([P, N], U32, align_bytes=64)
+        k_scales = keep.tile([P, N], U8, align_bytes=64)
+        q_codes = keep.tile([P, 2, NQ], U32, align_bytes=64)
+        q_scales = keep.tile([P, 2, NQ], U8, align_bytes=64)
+        v_codes = keep.tile([P, KV * E], U32, align_bytes=64)
+        v_scales = keep.tile([P, KV * E], U8, align_bytes=64)
+        neg_half = keep.tile([P, 2], F32)
+        warm = keep.tile([P, 2], F32)
+        sum_sq = keep.tile([P, UNITS], F32)
+        mean_sq = keep.tile([P, UNITS], F32)
+        rstd = keep.tile([P, UNITS], F32)
+        result = keep.tile([P, UNITS, E], F32)
+        score_banks = [psum.tile([P, PACK, QT], F32, name="scores%d" % b) for b in range(4)]
+        y_banks = [psum.tile([P, 2, E], F32, name="y%d" % b) for b in range(4)]
+
+        capped = {}
+        p_tiles = {}
+        w_bf = {}
+        w_mx = {}
+
+        k_view = kT.rearrange("g (p j) n -> (g p) j n", j=PACK)
+        q_mid = qT[1:3].rearrange("g (p j) n -> (g p) j n", j=PACK)
+        out_view = out.rearrange("h q e -> q h e")
+
+        def load_q_mid(c0, c1):
+            nc.sync.dma_start(out=q_raw[0][:, :, c0:c1], in_=q_mid[:, :, c0:c1])
+
+        def load_q_outer(g, c0, c1):
+            head = qT[HEAD_SETS[1][g]].rearrange("(p j) n -> p j n", j=PACK)
+            nc.sync.dma_start(out=q_raw[1][ROWS * g : ROWS * (g + 1), :, c0:c1], in_=head[:, :, c0:c1])
+
+        def interleave(copy, dst, src):
+            copy(out=dst.rearrange("p (c i) j -> p c j i", i=4), in_=src.rearrange("p j (c i) -> p c j i", i=4))
+
+        def quantize(codes, scales, src):
+            nc.vector.quantize_mx(out=codes.bitcast(FP8X4), scales=scales, in_=src.rearrange("p c j -> p (c j)"))
+
+        def copy_k(copy, c, s0, s1):
+            dst = k_bf[:, :, 64 * c + s0 : 64 * c + s1, :].rearrange("p r s j -> p s j r")
+            src = k_raw[c][:].rearrange("p j (s r) -> p s j r", r=PACK)[:, s0:s1, :, :]
+            copy(out=dst, in_=src)
+
+        def quantize_k(c):
+            for r in range(PACK):
+                cols = slice(P * r + 64 * c, P * r + 64 * (c + 1))
+                quantize(k_codes[:, cols], k_scales[:, cols], k_bf[:, r, 64 * c : 64 * (c + 1), :])
+
+        def copy_q(piece):
+            a, qt = divmod(piece, TILES)
+            cols = slice(QT * qt, QT * (qt + 1))
+            interleave(nc.vector.tensor_copy, q_bf[:, a, cols, :], q_raw[a][:, :, cols])
+
+        def quantize_q(piece):
+            a, qt = divmod(piece, TILES)
+            cols = slice(QT * qt, QT * (qt + 1))
+            quantize(q_codes[:, a, cols], q_scales[:, a, cols], q_bf[:, a, cols, :])
+
+        def scores(u):
+            piece, g = divmod(u, 2)
+            a, qt = divmod(piece, TILES)
+            rows = slice(ROWS * g, ROWS * (g + 1))
+            cols = slice(QT * qt, QT * (qt + 1))
+            for r in range(PACK):
+                tokens = slice(P * r, P * (r + 1))
+                nc.tensor.matmul_mx(
+                    out=score_banks[u % 4][:, r, :],
+                    lhsT=k_codes[rows, tokens].bitcast(FP8X4),
+                    lhsT_scale=k_scales[rows, tokens],
+                    rhs=q_codes[rows, a, cols].bitcast(FP8X4),
+                    rhs_scale=q_scales[rows, a, cols],
+                    start=True,
+                    stop=True,
+                )
+
+        def cap(u):
+            capped[u] = work.tile([P, QT, PACK], F32, name="capped")
+            nc.scalar.activation(
+                out=capped[u][:], in_=score_banks[u % 4][:].rearrange("p r q -> p q r"), func=ACT.Tanh, scale=0.5
+            )
+
+        def silu(u):
+            p_tiles[u] = work.tile([P, QT, PACK], F32, name="p")
+            nc.scalar.activation(out=p_tiles[u][:], in_=capped[u][:], func=ACT.Silu, scale=2.0)
+
+        def weigh(u):
+            w_bf[u] = work.tile([P, QT, PACK], BF16, name="w_bf", align_bytes=64)
+            nc.vector.tensor_tensor(
+                out=w_bf[u][:],
+                in0=p_tiles[u][:],
+                in1=t_sb[:].unsqueeze(1).to_broadcast([P, QT, PACK]),
+                op=ALU.mult,
+            )
+
+        def quantize_w(u):
+            codes = work.tile([P, QT], U32, name="w_codes", align_bytes=64)
+            scales = work.tile([P, QT], U8, name="w_scales", align_bytes=64)
+            w_mx[u] = (codes, scales)
+            quantize(codes[:], scales[:], w_bf[u][:])
+
+        def values(u):
+            cols = slice(E * (u % 2), E * (u % 2 + 1))
+            nc.tensor.matmul_mx(
+                out=y_banks[u // 2 % 4][:, u % 2, :],
+                lhsT=w_mx[u][0][:].bitcast(FP8X4),
+                lhsT_scale=w_mx[u][1][:],
+                rhs=v_codes[:, cols].bitcast(FP8X4),
+                rhs_scale=v_scales[:, cols],
+                start=True,
+                stop=True,
+            )
+
+        def square(u):
+            squares = work.tile([P, E], F32, name="squares")
+            nc.scalar.activation(
+                out=squares[:], in_=y_banks[u // 2 % 4][:, u % 2, :], func=ACT.Square, accum_out=sum_sq[:, u : u + 1]
+            )
+
+        def inverse_root(u0, u1):
+            nc.gpsimd.tensor_scalar(
+                out=mean_sq[:, u0:u1], in0=sum_sq[:, u0:u1], scalar1=1.0 / E, scalar2=EPS, op0=ALU.mult, op1=ALU.add
+            )
+            nc.gpsimd.tensor_tensor(out=rstd[:, u0:u1], in0=mean_sq[:, u0:u1], in1=neg_half[:, : u1 - u0], op=ALU.pow)
+
+        def normalise(u):
+            nc.vector.scalar_tensor_tensor(
+                out=result[:, u, :],
+                in0=y_banks[u // 2 % 4][:, u % 2, :],
+                scalar=rstd[:, u : u + 1],
+                in1=gn_sb[:],
+                op0=ALU.mult,
+                op1=ALU.mult,
+            )
+
+        def store(u0, u1):
+            piece = u0 // 2
+            a, qt = divmod(piece, TILES)
+            h0, h1 = HEAD_SETS[a]
+            rows = out_view[QT * qt : QT * (qt + 1), h0 : h1 + 1 : h1 - h0, :]
+            nc.sync.dma_start(out=rows[:, u0 % 2 : u0 % 2 + u1 - u0, :], in_=result[:, u0:u1, :])
+
+        load_q_mid(0, QT)
+        for c in range(2):
+            nc.sync.dma_start(out=k_raw[c][:], in_=k_view[:, :, HALF * c : HALF * (c + 1)])
+        nc.scalar.dma_start(out=t_sb[:], in_=t.rearrange("(p j) o -> p (j o)", j=PACK))
+        load_q_mid(QT, 2 * QT)
+        nc.sync.dma_start(
+            out=v_raw[:].rearrange("p g j e -> p g (j e)"), in_=v.rearrange("g (p j) e -> p g (j e)", j=PACK)
+        )
+        load_q_mid(2 * QT, NQ)
+        nc.sync.dma_start(out=gn_sb[:], in_=gn[:, :])
+        for half in range(2):
+            for g in range(2):
+                load_q_outer(g, 2 * QT * half, 2 * QT * (half + 1))
+
+        nc.gpsimd.memset(neg_half[:], -0.5)
+        nc.scalar.activation(out=warm[:], in_=neg_half[:], func=ACT.Silu)
+
+        copy_q(0)
+        copy_k(nc.scalar.copy, 0, K_SPLIT, 64)
+        copy_k(nc.vector.tensor_copy, 0, 0, K_SPLIT)
+        quantize_q(0)
+        quantize_k(0)
+        copy_k(nc.scalar.copy, 1, K_SPLIT, 64)
+        copy_k(nc.vector.tensor_copy, 1, 0, K_SPLIT)
+        quantize_k(1)
+        scores(0)
+        scores(1)
+        copy_q(1)
+        interleave(nc.vector.tensor_copy, v_bf[:, 0, :, :], v_raw[:, 0, :, :])
+        quantize_q(1)
+        interleave(nc.vector.tensor_copy, v_bf[:, 1, :, :], v_raw[:, 1, :, :])
+        copy_q(2)
+        quantize(v_codes[:], v_scales[:], v_bf[:].rearrange("p g e j -> p (g e) j"))
+        cap(0)
+
+        quantize_at = {0: 2, 1: 3, 4: 4, 6: 5, 8: 6, 10: 7}
+        copy_at = {0: 3, 3: 4, 5: 5, 7: 6, 9: 7}
+        last = UNITS - 1
+        for s in range(UNITS):
+            if s + 2 <= last:
+                scores(s + 2)
+            if s + 1 <= last:
+                cap(s + 1)
+            silu(s)
+            if s >= 3:
+                square(s - 3)
+                if s % 2 == 0:
+                    inverse_root(s - 4, s - 2)
+            weigh(s)
+            if s in quantize_at:
+                quantize_q(quantize_at[s])
+            if s >= 6:
+                normalise(s - 6)
+                if s % 2 == 1:
+                    store(s - 7, s - 5)
+            quantize_w(s)
+            values(s)
+            if s in copy_at:
+                copy_q(copy_at[s])
+        square(13)
+        inverse_root(12, 14)
+        normalise(10)
+        normalise(11)
+        store(10, 12)
+        square(14)
+        square(15)
+        inverse_root(14, 16)
+        normalise(12)
+        normalise(13)
+        store(12, 14)
+        normalise(14)
+        normalise(15)
+        store(14, 16)

@@ -23,6 +23,7 @@ HALF = N // 2
 EPS = 1e-5 * 256.0
 HEAD_SETS = ((1, 2), (0, 3))
 K_SPLIT = 40
+Q_SPLIT = 64
 
 
 def tile_rows_a_silu_cap_onorm_kernel(tc, qT, kT, t, v, gn, out):
@@ -121,24 +122,27 @@ def tile_rows_a_silu_cap_onorm_kernel(tc, qT, kT, t, v, gn, out):
                 out=capped[u][:], in_=score_banks[u % 4][:].rearrange("p r q -> p q r"), func=ACT.Tanh, scale=0.5
             )
 
-        def silu(u):
-            p_tiles[u] = work.tile([P, QT, PACK], F32, name="p")
-            nc.scalar.activation(out=p_tiles[u][:], in_=capped[u][:], func=ACT.Silu, scale=2.0)
+        def silu(u, c0=0, c1=QT):
+            if c0 == 0:
+                p_tiles[u] = work.tile([P, QT, PACK], F32, name="p")
+            nc.scalar.activation(out=p_tiles[u][:, c0:c1, :], in_=capped[u][:, c0:c1, :], func=ACT.Silu, scale=2.0)
 
-        def weigh(u):
-            w_bf[u] = work.tile([P, QT, PACK], BF16, name="w_bf", align_bytes=64)
+        def weigh(u, c0=0, c1=QT):
+            if c0 == 0:
+                w_bf[u] = work.tile([P, QT, PACK], BF16, name="w_bf", align_bytes=64)
             nc.vector.tensor_tensor(
-                out=w_bf[u][:],
-                in0=p_tiles[u][:],
-                in1=t_sb[:].unsqueeze(1).to_broadcast([P, QT, PACK]),
+                out=w_bf[u][:, c0:c1, :],
+                in0=p_tiles[u][:, c0:c1, :],
+                in1=t_sb[:].unsqueeze(1).to_broadcast([P, c1 - c0, PACK]),
                 op=ALU.mult,
             )
 
-        def quantize_w(u):
-            codes = work.tile([P, QT], U32, name="w_codes", align_bytes=64)
-            scales = work.tile([P, QT], U8, name="w_scales", align_bytes=64)
-            w_mx[u] = (codes, scales)
-            quantize(codes[:], scales[:], w_bf[u][:])
+        def quantize_w(u, c0=0, c1=QT):
+            if c0 == 0:
+                codes = work.tile([P, QT], U32, name="w_codes", align_bytes=64)
+                scales = work.tile([P, QT], U8, name="w_scales", align_bytes=64)
+                w_mx[u] = (codes, scales)
+            quantize(w_mx[u][0][:, c0:c1], w_mx[u][1][:, c0:c1], w_bf[u][:, c0:c1, :])
 
         def values(u):
             cols = slice(E * (u % 2), E * (u % 2 + 1))
@@ -181,9 +185,9 @@ def tile_rows_a_silu_cap_onorm_kernel(tc, qT, kT, t, v, gn, out):
             rows = out_view[QT * qt : QT * (qt + 1), h0 : h1 + 1 : h1 - h0, :]
             nc.sync.dma_start(out=rows[:, u0 % 2 : u0 % 2 + u1 - u0, :], in_=result[:, u0:u1, :])
 
-        load_q_mid(0, QT)
         for c in range(2):
             nc.sync.dma_start(out=k_raw[c][:], in_=k_view[:, :, HALF * c : HALF * (c + 1)])
+        load_q_mid(0, QT)
         nc.scalar.dma_start(out=t_sb[:], in_=t.rearrange("(p j) o -> p (j o)", j=PACK))
         load_q_mid(QT, 2 * QT)
         nc.sync.dma_start(
@@ -198,20 +202,20 @@ def tile_rows_a_silu_cap_onorm_kernel(tc, qT, kT, t, v, gn, out):
         nc.gpsimd.memset(neg_half[:], -0.5)
         nc.scalar.activation(out=warm[:], in_=neg_half[:], func=ACT.Silu)
 
-        copy_q(0)
-        copy_k(nc.scalar.copy, 0, K_SPLIT, 64)
-        copy_k(nc.vector.tensor_copy, 0, 0, K_SPLIT)
+        for c in range(2):
+            copy_k(nc.scalar.copy, c, K_SPLIT, 64)
+            copy_k(nc.vector.tensor_copy, c, 0, K_SPLIT)
+            quantize_k(c)
+        interleave(nc.scalar.copy, q_bf[:, 0, :Q_SPLIT, :], q_raw[0][:, :, :Q_SPLIT])
+        interleave(nc.vector.tensor_copy, q_bf[:, 0, Q_SPLIT:QT, :], q_raw[0][:, :, Q_SPLIT:QT])
         quantize_q(0)
-        quantize_k(0)
-        copy_k(nc.scalar.copy, 1, K_SPLIT, 64)
-        copy_k(nc.vector.tensor_copy, 1, 0, K_SPLIT)
-        quantize_k(1)
         scores(0)
         scores(1)
         copy_q(1)
         interleave(nc.vector.tensor_copy, v_bf[:, 0, :, :], v_raw[:, 0, :, :])
         quantize_q(1)
         interleave(nc.vector.tensor_copy, v_bf[:, 1, :, :], v_raw[:, 1, :, :])
+        scores(2)
         copy_q(2)
         quantize(v_codes[:], v_scales[:], v_bf[:].rearrange("p g e j -> p (g e) j"))
         cap(0)
@@ -219,9 +223,11 @@ def tile_rows_a_silu_cap_onorm_kernel(tc, qT, kT, t, v, gn, out):
         quantize_at = {0: 2, 1: 3, 4: 4, 6: 5, 8: 6, 10: 7}
         copy_at = {0: 3, 3: 4, 5: 5, 7: 6, 9: 7}
         last = UNITS - 1
-        for s in range(UNITS):
-            if s + 2 <= last:
-                scores(s + 2)
+        for s in range(last):
+            if s + 3 <= last:
+                scores(s + 3)
+            if s >= 1:
+                values(s - 1)
             if s + 1 <= last:
                 cap(s + 1)
             silu(s)
@@ -236,21 +242,33 @@ def tile_rows_a_silu_cap_onorm_kernel(tc, qT, kT, t, v, gn, out):
                 normalise(s - 6)
                 if s % 2 == 1:
                     store(s - 7, s - 5)
-            quantize_w(s)
-            values(s)
             if s in copy_at:
                 copy_q(copy_at[s])
+            quantize_w(s)
+        values(14)
+        silu(15, 0, 64)
+        silu(15, 64, QT)
+        square(12)
         square(13)
         inverse_root(12, 14)
+        square(14)
+        inverse_root(14, 15)
+        weigh(15, 0, 64)
+        normalise(9)
+        store(8, 10)
+        weigh(15, 64, QT)
+        quantize_w(15, 0, 64)
         normalise(10)
+        quantize_w(15, 64, QT)
+        values(15)
         normalise(11)
         store(10, 12)
-        square(14)
         square(15)
-        inverse_root(14, 16)
+        inverse_root(15, 16)
         normalise(12)
         normalise(13)
         store(12, 14)
         normalise(14)
+        store(14, 15)
         normalise(15)
-        store(14, 16)
+        store(15, 16)

@@ -22,8 +22,7 @@ UNITS = H * TILES
 HALF = N // 2
 EPS = 1e-5 * 256.0
 HEAD_SETS = ((1, 2), (0, 3))
-K_SPLIT = 40
-Q_SPLIT = 64
+K_SPLIT = 44
 
 
 def tile_rows_a_silu_cap_onorm_kernel(tc, qT, kT, t, v, gn, out):
@@ -48,14 +47,14 @@ def tile_rows_a_silu_cap_onorm_kernel(tc, qT, kT, t, v, gn, out):
         q_scales = keep.tile([P, 2, NQ], U8, align_bytes=64)
         v_codes = keep.tile([P, KV * E], U32, align_bytes=64)
         v_scales = keep.tile([P, KV * E], U8, align_bytes=64)
-        neg_half = keep.tile([P, 2], F32)
+        neg_half = keep.tile([P, 4], F32)
         warm = keep.tile([P, 2], F32)
         sum_sq = keep.tile([P, UNITS], F32)
         mean_sq = keep.tile([P, UNITS], F32)
         rstd = keep.tile([P, UNITS], F32)
         result = keep.tile([P, UNITS, E], F32)
-        score_banks = [psum.tile([P, PACK, QT], F32, name="scores%d" % b) for b in range(4)]
-        y_banks = [psum.tile([P, 2, E], F32, name="y%d" % b) for b in range(4)]
+        score_banks = [psum.tile([P, PACK, QT], F32, name="scores%d" % b) for b in range(2)]
+        y_banks = [psum.tile([P, E], F32, name="y%d" % b) for b in range(6)]
 
         capped = {}
         p_tiles = {}
@@ -107,7 +106,7 @@ def tile_rows_a_silu_cap_onorm_kernel(tc, qT, kT, t, v, gn, out):
             for r in range(PACK):
                 tokens = slice(P * r, P * (r + 1))
                 nc.tensor.matmul_mx(
-                    out=score_banks[u % 4][:, r, :],
+                    out=score_banks[u % 2][:, r, :],
                     lhsT=k_codes[rows, tokens].bitcast(FP8X4),
                     lhsT_scale=k_scales[rows, tokens],
                     rhs=q_codes[rows, a, cols].bitcast(FP8X4),
@@ -119,7 +118,7 @@ def tile_rows_a_silu_cap_onorm_kernel(tc, qT, kT, t, v, gn, out):
         def cap(u):
             capped[u] = work.tile([P, QT, PACK], F32, name="capped")
             nc.scalar.activation(
-                out=capped[u][:], in_=score_banks[u % 4][:].rearrange("p r q -> p q r"), func=ACT.Tanh, scale=0.5
+                out=capped[u][:], in_=score_banks[u % 2][:].rearrange("p r q -> p q r"), func=ACT.Tanh, scale=0.5
             )
 
         def silu(u, c0=0, c1=QT):
@@ -147,7 +146,7 @@ def tile_rows_a_silu_cap_onorm_kernel(tc, qT, kT, t, v, gn, out):
         def values(u):
             cols = slice(E * (u % 2), E * (u % 2 + 1))
             nc.tensor.matmul_mx(
-                out=y_banks[u // 2 % 4][:, u % 2, :],
+                out=y_banks[u % 6][:],
                 lhsT=w_mx[u][0][:].bitcast(FP8X4),
                 lhsT_scale=w_mx[u][1][:],
                 rhs=v_codes[:, cols].bitcast(FP8X4),
@@ -159,11 +158,11 @@ def tile_rows_a_silu_cap_onorm_kernel(tc, qT, kT, t, v, gn, out):
         def square(u):
             squares = work.tile([P, E], F32, name="squares")
             nc.scalar.activation(
-                out=squares[:], in_=y_banks[u // 2 % 4][:, u % 2, :], func=ACT.Square, accum_out=sum_sq[:, u : u + 1]
+                out=squares[:], in_=y_banks[u % 6][:], func=ACT.Square, accum_out=sum_sq[:, u : u + 1]
             )
 
         def inverse_root(u0, u1):
-            nc.gpsimd.tensor_scalar(
+            nc.vector.tensor_scalar(
                 out=mean_sq[:, u0:u1], in0=sum_sq[:, u0:u1], scalar1=1.0 / E, scalar2=EPS, op0=ALU.mult, op1=ALU.add
             )
             nc.gpsimd.tensor_tensor(out=rstd[:, u0:u1], in0=mean_sq[:, u0:u1], in1=neg_half[:, : u1 - u0], op=ALU.pow)
@@ -171,7 +170,7 @@ def tile_rows_a_silu_cap_onorm_kernel(tc, qT, kT, t, v, gn, out):
         def normalise(u):
             nc.vector.scalar_tensor_tensor(
                 out=result[:, u, :],
-                in0=y_banks[u // 2 % 4][:, u % 2, :],
+                in0=y_banks[u % 6][:],
                 scalar=rstd[:, u : u + 1],
                 in1=gn_sb[:],
                 op0=ALU.mult,
@@ -185,9 +184,9 @@ def tile_rows_a_silu_cap_onorm_kernel(tc, qT, kT, t, v, gn, out):
             rows = out_view[QT * qt : QT * (qt + 1), h0 : h1 + 1 : h1 - h0, :]
             nc.sync.dma_start(out=rows[:, u0 % 2 : u0 % 2 + u1 - u0, :], in_=result[:, u0:u1, :])
 
+        load_q_mid(0, QT)
         for c in range(2):
             nc.sync.dma_start(out=k_raw[c][:], in_=k_view[:, :, HALF * c : HALF * (c + 1)])
-        load_q_mid(0, QT)
         nc.scalar.dma_start(out=t_sb[:], in_=t.rearrange("(p j) o -> p (j o)", j=PACK))
         load_q_mid(QT, 2 * QT)
         nc.sync.dma_start(
@@ -200,70 +199,86 @@ def tile_rows_a_silu_cap_onorm_kernel(tc, qT, kT, t, v, gn, out):
                 load_q_outer(g, 2 * QT * half, 2 * QT * (half + 1))
 
         nc.gpsimd.memset(neg_half[:], -0.5)
-        nc.scalar.activation(out=warm[:], in_=neg_half[:], func=ACT.Silu)
+        nc.scalar.activation(out=warm[:], in_=neg_half[:, :2], func=ACT.Silu)
 
+        copy_q(0)
         for c in range(2):
             copy_k(nc.scalar.copy, c, K_SPLIT, 64)
             copy_k(nc.vector.tensor_copy, c, 0, K_SPLIT)
+            if c == 0:
+                quantize_q(0)
             quantize_k(c)
-        interleave(nc.scalar.copy, q_bf[:, 0, :Q_SPLIT, :], q_raw[0][:, :, :Q_SPLIT])
-        interleave(nc.vector.tensor_copy, q_bf[:, 0, Q_SPLIT:QT, :], q_raw[0][:, :, Q_SPLIT:QT])
-        quantize_q(0)
         scores(0)
         scores(1)
         copy_q(1)
         interleave(nc.vector.tensor_copy, v_bf[:, 0, :, :], v_raw[:, 0, :, :])
         quantize_q(1)
         interleave(nc.vector.tensor_copy, v_bf[:, 1, :, :], v_raw[:, 1, :, :])
-        scores(2)
         copy_q(2)
         quantize(v_codes[:], v_scales[:], v_bf[:].rearrange("p g e j -> p (g e) j"))
+        quantize_q(2)
         cap(0)
+        cap(1)
 
-        quantize_at = {0: 2, 1: 3, 4: 4, 6: 5, 8: 6, 10: 7}
-        copy_at = {0: 3, 3: 4, 5: 5, 7: 6, 9: 7}
-        last = UNITS - 1
-        for s in range(last):
-            if s + 3 <= last:
-                scores(s + 3)
-            if s >= 1:
-                values(s - 1)
-            if s + 1 <= last:
-                cap(s + 1)
-            silu(s)
-            if s >= 3:
-                square(s - 3)
-                if s % 2 == 0:
-                    inverse_root(s - 4, s - 2)
-            weigh(s)
-            if s in quantize_at:
-                quantize_q(quantize_at[s])
-            if s >= 6:
-                normalise(s - 6)
-                if s % 2 == 1:
-                    store(s - 7, s - 5)
-            if s in copy_at:
-                copy_q(copy_at[s])
-            quantize_w(s)
+        for i in range(7):
+            a, b = 2 * i, 2 * i + 1
+            scores(a + 2)
+            scores(b + 2)
+            if i >= 1:
+                values(a - 2)
+                values(b - 2)
+            silu(a)
+            silu(b)
+            if i >= 2:
+                square(a - 4)
+                square(b - 4)
+            cap(a + 2)
+            cap(b + 2)
+            weigh(a)
+            if i >= 5:
+                inverse_root(a - 4, a - 2)
+                weigh(b)
+                normalise(a - 6)
+                normalise(b - 6)
+                store(a - 6, a - 4)
+                quantize_w(a)
+                quantize_w(b)
+                continue
+            weigh(b)
+            copy_q(i + 3)
+            quantize_w(a)
+            if i >= 2:
+                inverse_root(a - 4, a - 2)
+            if i >= 3:
+                normalise(a - 6)
+            quantize_w(b)
+            if i >= 3:
+                normalise(b - 6)
+                store(a - 6, a - 4)
+            quantize_q(i + 3)
+        values(12)
+        values(13)
+        silu(14)
+        silu(15)
+        for u in range(10, 14):
+            square(u)
+        weigh(14)
+        weigh(15)
+        normalise(8)
+        quantize_w(14)
         values(14)
-        silu(15, 0, 64)
-        silu(15, 64, QT)
-        square(12)
-        square(13)
-        inverse_root(12, 14)
         square(14)
-        inverse_root(14, 15)
-        weigh(15, 0, 64)
         normalise(9)
         store(8, 10)
-        weigh(15, 64, QT)
-        quantize_w(15, 0, 64)
-        normalise(10)
-        quantize_w(15, 64, QT)
+        inverse_root(10, 12)
+        quantize_w(15)
         values(15)
+        square(15)
+        inverse_root(12, 14)
+        inverse_root(14, 15)
+        normalise(10)
         normalise(11)
         store(10, 12)
-        square(15)
         inverse_root(15, 16)
         normalise(12)
         normalise(13)

@@ -29,7 +29,7 @@ def tile_rows_a_silu_cap_onorm_kernel(tc, qT, kT, t, v, gn, out):
     nc = tc.nc
     with ExitStack() as ctx:
         keep = ctx.enter_context(tc.tile_pool(name="keep", bufs=1))
-        work = ctx.enter_context(tc.tile_pool(name="work", bufs=4))
+        work = ctx.enter_context(tc.tile_pool(name="work", bufs=UNITS))
         psum = ctx.enter_context(tc.psum_pool(name="psum", bufs=1))
         ctx.enter_context(tc.manual_schedule())
 
@@ -52,6 +52,9 @@ def tile_rows_a_silu_cap_onorm_kernel(tc, qT, kT, t, v, gn, out):
         sum_sq = keep.tile([P, UNITS], F32)
         mean_sq = keep.tile([P, UNITS], F32)
         rstd = keep.tile([P, UNITS], F32)
+        stats = keep.tile([P, UNITS, 6], F32)
+        half_mean_sq = keep.tile([P, UNITS, 2], F32)
+        parts = keep.tile([P, UNITS, 2], F32)
         result = keep.tile([P, UNITS, E], F32)
         score_banks = [psum.tile([P, PACK, QT], F32, name="scores%d" % b) for b in range(2)]
         y_banks = [psum.tile([P, E], F32, name="y%d" % b) for b in range(6)]
@@ -161,11 +164,44 @@ def tile_rows_a_silu_cap_onorm_kernel(tc, qT, kT, t, v, gn, out):
                 out=squares[:], in_=y_banks[u % 6][:], func=ACT.Square, accum_out=sum_sq[:, u : u + 1]
             )
 
+        def statistics(u):
+            nc.vector.bn_stats(out=stats[:, u, :], in_=y_banks[u % 6][:])
+
+        def square_means(u0, u1):
+            means = stats[:, u0:u1, 1:6:3]
+            nc.vector.scalar_tensor_tensor(
+                out=half_mean_sq[:, u0:u1, :], in0=means, scalar=0.5, in1=means, op0=ALU.mult, op1=ALU.mult
+            )
+
+        def add_spread(u0, u1):
+            nc.vector.scalar_tensor_tensor(
+                out=parts[:, u0:u1, :],
+                in0=stats[:, u0:u1, 2:6:3],
+                scalar=1.0 / E,
+                in1=half_mean_sq[:, u0:u1, :],
+                op0=ALU.mult,
+                op1=ALU.add,
+            )
+
+        def root(u0, u1):
+            nc.gpsimd.tensor_tensor(out=rstd[:, u0:u1], in0=mean_sq[:, u0:u1], in1=neg_half[:, : u1 - u0], op=ALU.pow)
+
+        def inverse_root_of_parts(u0, u1):
+            nc.vector.scalar_tensor_tensor(
+                out=mean_sq[:, u0:u1],
+                in0=parts[:, u0:u1, 0],
+                scalar=EPS,
+                in1=parts[:, u0:u1, 1],
+                op0=ALU.add,
+                op1=ALU.add,
+            )
+            root(u0, u1)
+
         def inverse_root(u0, u1):
             nc.vector.tensor_scalar(
                 out=mean_sq[:, u0:u1], in0=sum_sq[:, u0:u1], scalar1=1.0 / E, scalar2=EPS, op0=ALU.mult, op1=ALU.add
             )
-            nc.gpsimd.tensor_tensor(out=rstd[:, u0:u1], in0=mean_sq[:, u0:u1], in1=neg_half[:, : u1 - u0], op=ALU.pow)
+            root(u0, u1)
 
         def normalise(u):
             nc.vector.scalar_tensor_tensor(
@@ -193,10 +229,11 @@ def tile_rows_a_silu_cap_onorm_kernel(tc, qT, kT, t, v, gn, out):
             out=v_raw[:].rearrange("p g j e -> p g (j e)"), in_=v.rearrange("g (p j) e -> p g (j e)", j=PACK)
         )
         load_q_mid(2 * QT, NQ)
-        nc.sync.dma_start(out=gn_sb[:], in_=gn[:, :])
         for half in range(2):
             for g in range(2):
                 load_q_outer(g, 2 * QT * half, 2 * QT * (half + 1))
+            if half == 0:
+                nc.sync.dma_start(out=gn_sb[:], in_=gn[:, :])
 
         nc.gpsimd.memset(neg_half[:], -0.5)
         nc.scalar.activation(out=warm[:], in_=neg_half[:, :2], func=ACT.Silu)
@@ -215,6 +252,7 @@ def tile_rows_a_silu_cap_onorm_kernel(tc, qT, kT, t, v, gn, out):
         quantize_q(1)
         interleave(nc.vector.tensor_copy, v_bf[:, 1, :, :], v_raw[:, 1, :, :])
         copy_q(2)
+        copy_q(3)
         quantize(v_codes[:], v_scales[:], v_bf[:].rearrange("p g e j -> p (g e) j"))
         quantize_q(2)
         cap(0)
@@ -229,33 +267,29 @@ def tile_rows_a_silu_cap_onorm_kernel(tc, qT, kT, t, v, gn, out):
                 values(b - 2)
             silu(a)
             silu(b)
-            if i >= 2:
-                square(a - 4)
-                square(b - 4)
             cap(a + 2)
             cap(b + 2)
             weigh(a)
-            if i >= 5:
-                inverse_root(a - 4, a - 2)
-                weigh(b)
-                normalise(a - 6)
-                normalise(b - 6)
-                store(a - 6, a - 4)
-                quantize_w(a)
-                quantize_w(b)
-                continue
-            weigh(b)
-            copy_q(i + 3)
-            quantize_w(a)
             if i >= 2:
-                inverse_root(a - 4, a - 2)
+                add_spread(a - 4, a - 2)
+            weigh(b)
+            if i >= 2:
+                inverse_root_of_parts(a - 4, a - 2)
+            quantize_w(a)
+            if 1 <= i <= 5:
+                statistics(a - 2)
+                statistics(b - 2)
             if i >= 3:
                 normalise(a - 6)
-            quantize_w(b)
-            if i >= 3:
                 normalise(b - 6)
                 store(a - 6, a - 4)
-            quantize_q(i + 3)
+            quantize_w(b)
+            if 1 <= i <= 5:
+                square_means(a - 2, a)
+            if i <= 4:
+                quantize_q(i + 3)
+            if i <= 3:
+                copy_q(i + 4)
         values(12)
         values(13)
         silu(14)
@@ -270,13 +304,13 @@ def tile_rows_a_silu_cap_onorm_kernel(tc, qT, kT, t, v, gn, out):
         square(14)
         normalise(9)
         store(8, 10)
-        inverse_root(10, 12)
         quantize_w(15)
         values(15)
         square(15)
+        inverse_root(10, 12)
         inverse_root(12, 14)
-        inverse_root(14, 15)
         normalise(10)
+        inverse_root(14, 15)
         normalise(11)
         store(10, 12)
         inverse_root(15, 16)

@@ -1,3 +1,4 @@
+import math
 from contextlib import ExitStack
 
 import concourse.mybir as mybir
@@ -19,10 +20,18 @@ PACK = 4
 QT = 128
 TILES = NQ // QT
 UNITS = H * TILES
-HALF = N // 2
-EPS = 1e-5 * 256.0
+PAIRS = UNITS // 2
+BANKS = 4
+
 HEAD_SETS = ((1, 2), (0, 3))
-K_SPLIT = 44
+
+KEY_HALF = N // 2
+S_HALF = KEY_HALF // PACK
+S_VECTOR = 44
+
+SUM_EPS = E * 1e-5 * 16.0**2
+
+FIRST_SCALAR_PAIR = 5
 
 
 def tile_rows_a_silu_cap_onorm_kernel(tc, qT, kT, t, v, gn, out):
@@ -33,10 +42,11 @@ def tile_rows_a_silu_cap_onorm_kernel(tc, qT, kT, t, v, gn, out):
         psum = ctx.enter_context(tc.psum_pool(name="psum", bufs=1))
         ctx.enter_context(tc.manual_schedule())
 
-        k_raw = [keep.tile([P, PACK, HALF], F32, name="k_raw%d" % c) for c in range(2)]
-        q_raw = [keep.tile([P, PACK, NQ], F32, name="q_raw%d" % a) for a in range(2)]
+        k_raw = [keep.tile([P, PACK, KEY_HALF], F32, name="k_raw%d" % c) for c in range(2)]
+        q_raw = [keep.tile([P, PACK, NQ], F32, name="q_raw%d" % hs) for hs in range(2)]
         v_raw = keep.tile([P, KV, PACK, E], F32)
         t_sb = keep.tile([P, PACK], F32)
+        t_wide = keep.tile([P, QT, PACK], F32)
         gn_sb = keep.tile([P, E], F32)
         k_bf = keep.tile([P, PACK, P, PACK], BF16, align_bytes=64)
         q_bf = keep.tile([P, 2, NQ, PACK], BF16, align_bytes=64)
@@ -47,73 +57,76 @@ def tile_rows_a_silu_cap_onorm_kernel(tc, qT, kT, t, v, gn, out):
         q_scales = keep.tile([P, 2, NQ], U8, align_bytes=64)
         v_codes = keep.tile([P, KV * E], U32, align_bytes=64)
         v_scales = keep.tile([P, KV * E], U8, align_bytes=64)
-        neg_half = keep.tile([P, 4], F32)
+        neg_half = keep.tile([P, 2], F32)
         warm = keep.tile([P, 2], F32)
+        stats = keep.tile([P, PAIRS, 6], F32)
+        mean_part = keep.tile([P, PAIRS, 2], F32)
         sum_sq = keep.tile([P, UNITS], F32)
-        mean_sq = keep.tile([P, UNITS], F32)
+        radicand = keep.tile([P, UNITS], F32)
         rstd = keep.tile([P, UNITS], F32)
-        stats = keep.tile([P, UNITS, 6], F32)
-        half_mean_sq = keep.tile([P, UNITS, 2], F32)
-        parts = keep.tile([P, UNITS, 2], F32)
+        gain = keep.tile([P, E], F32)
         result = keep.tile([P, UNITS, E], F32)
-        score_banks = [psum.tile([P, PACK, QT], F32, name="scores%d" % b) for b in range(2)]
-        y_banks = [psum.tile([P, E], F32, name="y%d" % b) for b in range(6)]
+        score_banks = [psum.tile([P, PACK, QT], F32, name="scores%d" % n) for n in range(BANKS)]
+        y_banks = [psum.tile([P, 2, E], F32, name="y%d" % n) for n in range(BANKS)]
 
-        capped = {}
-        p_tiles = {}
-        w_bf = {}
-        w_mx = {}
+        capped, p_tiles, w_bf, w_mx = {}, {}, {}, {}
 
         k_view = kT.rearrange("g (p j) n -> (g p) j n", j=PACK)
-        q_mid = qT[1:3].rearrange("g (p j) n -> (g p) j n", j=PACK)
+        q_first = qT[HEAD_SETS[0][0] : HEAD_SETS[0][1] + 1].rearrange("g (p j) n -> (g p) j n", j=PACK)
         out_view = out.rearrange("h q e -> q h e")
 
-        def load_q_mid(c0, c1):
-            nc.sync.dma_start(out=q_raw[0][:, :, c0:c1], in_=q_mid[:, :, c0:c1])
+        def y_of(u):
+            if u == UNITS - 1:
+                return y_banks[0][:, 0, :]
+            return y_banks[u // 2 % BANKS][:, u % 2, :]
 
-        def load_q_outer(g, c0, c1):
-            head = qT[HEAD_SETS[1][g]].rearrange("(p j) n -> p j n", j=PACK)
-            nc.sync.dma_start(out=q_raw[1][ROWS * g : ROWS * (g + 1), :, c0:c1], in_=head[:, :, c0:c1])
+        def load_first_set(c0, c1):
+            nc.sync.dma_start(out=q_raw[0][:, :, c0:c1], in_=q_first[:, :, c0:c1])
 
-        def interleave(copy, dst, src):
-            copy(out=dst.rearrange("p (c i) j -> p c j i", i=4), in_=src.rearrange("p j (c i) -> p c j i", i=4))
+        def load_second_set(c0, c1):
+            for g in range(KV):
+                head = qT[HEAD_SETS[1][g]].rearrange("(p j) n -> p j n", j=PACK)
+                nc.sync.dma_start(out=q_raw[1][ROWS * g : ROWS * (g + 1), :, c0:c1], in_=head[:, :, c0:c1])
+
+        def interleave(dst, src):
+            nc.vector.tensor_copy(
+                out=dst.rearrange("p (c x) j -> p c j x", x=4), in_=src.rearrange("p j (c x) -> p c j x", x=4)
+            )
 
         def quantize(codes, scales, src):
             nc.vector.quantize_mx(out=codes.bitcast(FP8X4), scales=scales, in_=src.rearrange("p c j -> p (c j)"))
 
         def copy_k(copy, c, s0, s1):
-            dst = k_bf[:, :, 64 * c + s0 : 64 * c + s1, :].rearrange("p r s j -> p s j r")
-            src = k_raw[c][:].rearrange("p j (s r) -> p s j r", r=PACK)[:, s0:s1, :, :]
-            copy(out=dst, in_=src)
+            dst = k_bf[:, :, S_HALF * c + s0 : S_HALF * c + s1, :].rearrange("p r s j -> p s j r")
+            copy(out=dst, in_=k_raw[c][:].rearrange("p j (s r) -> p s j r", r=PACK)[:, s0:s1, :, :])
 
         def quantize_k(c):
             for r in range(PACK):
-                cols = slice(P * r + 64 * c, P * r + 64 * (c + 1))
-                quantize(k_codes[:, cols], k_scales[:, cols], k_bf[:, r, 64 * c : 64 * (c + 1), :])
+                cols = slice(P * r + S_HALF * c, P * r + S_HALF * (c + 1))
+                quantize(k_codes[:, cols], k_scales[:, cols], k_bf[:, r, S_HALF * c : S_HALF * (c + 1), :])
 
-        def copy_q(piece):
-            a, qt = divmod(piece, TILES)
+        def copy_q(i):
+            hs, qt = divmod(i, TILES)
             cols = slice(QT * qt, QT * (qt + 1))
-            interleave(nc.vector.tensor_copy, q_bf[:, a, cols, :], q_raw[a][:, :, cols])
+            interleave(q_bf[:, hs, cols, :], q_raw[hs][:, :, cols])
 
-        def quantize_q(piece):
-            a, qt = divmod(piece, TILES)
+        def quantize_q(i):
+            hs, qt = divmod(i, TILES)
             cols = slice(QT * qt, QT * (qt + 1))
-            quantize(q_codes[:, a, cols], q_scales[:, a, cols], q_bf[:, a, cols, :])
+            quantize(q_codes[:, hs, cols], q_scales[:, hs, cols], q_bf[:, hs, cols, :])
 
         def scores(u):
-            piece, g = divmod(u, 2)
-            a, qt = divmod(piece, TILES)
-            rows = slice(ROWS * g, ROWS * (g + 1))
+            hs, qt = divmod(u // 2, TILES)
+            rows = slice(ROWS * (u % 2), ROWS * (u % 2 + 1))
             cols = slice(QT * qt, QT * (qt + 1))
             for r in range(PACK):
                 tokens = slice(P * r, P * (r + 1))
                 nc.tensor.matmul_mx(
-                    out=score_banks[u % 2][:, r, :],
+                    out=score_banks[u % BANKS][:, r, :],
                     lhsT=k_codes[rows, tokens].bitcast(FP8X4),
                     lhsT_scale=k_scales[rows, tokens],
-                    rhs=q_codes[rows, a, cols].bitcast(FP8X4),
-                    rhs_scale=q_scales[rows, a, cols],
+                    rhs=q_codes[rows, hs, cols].bitcast(FP8X4),
+                    rhs_scale=q_scales[rows, hs, cols],
                     start=True,
                     stop=True,
                 )
@@ -121,35 +134,27 @@ def tile_rows_a_silu_cap_onorm_kernel(tc, qT, kT, t, v, gn, out):
         def cap(u):
             capped[u] = work.tile([P, QT, PACK], F32, name="capped")
             nc.scalar.activation(
-                out=capped[u][:], in_=score_banks[u % 2][:].rearrange("p r q -> p q r"), func=ACT.Tanh, scale=0.5
+                out=capped[u][:], in_=score_banks[u % BANKS][:].rearrange("p r q -> p q r"), func=ACT.Tanh, scale=0.5
             )
 
-        def silu(u, c0=0, c1=QT):
-            if c0 == 0:
-                p_tiles[u] = work.tile([P, QT, PACK], F32, name="p")
-            nc.scalar.activation(out=p_tiles[u][:, c0:c1, :], in_=capped[u][:, c0:c1, :], func=ACT.Silu, scale=2.0)
+        def silu(u):
+            p_tiles[u] = work.tile([P, QT, PACK], F32, name="p")
+            nc.scalar.activation(out=p_tiles[u][:], in_=capped[u][:], func=ACT.Silu, scale=2.0)
 
-        def weigh(u, c0=0, c1=QT):
-            if c0 == 0:
-                w_bf[u] = work.tile([P, QT, PACK], BF16, name="w_bf", align_bytes=64)
-            nc.vector.tensor_tensor(
-                out=w_bf[u][:, c0:c1, :],
-                in0=p_tiles[u][:, c0:c1, :],
-                in1=t_sb[:].unsqueeze(1).to_broadcast([P, c1 - c0, PACK]),
-                op=ALU.mult,
-            )
+        def weigh(u):
+            w_bf[u] = work.tile([P, QT, PACK], BF16, name="w_bf", align_bytes=64)
+            nc.vector.tensor_tensor(out=w_bf[u][:], in0=p_tiles[u][:], in1=t_wide[:], op=ALU.mult)
 
-        def quantize_w(u, c0=0, c1=QT):
-            if c0 == 0:
-                codes = work.tile([P, QT], U32, name="w_codes", align_bytes=64)
-                scales = work.tile([P, QT], U8, name="w_scales", align_bytes=64)
-                w_mx[u] = (codes, scales)
-            quantize(w_mx[u][0][:, c0:c1], w_mx[u][1][:, c0:c1], w_bf[u][:, c0:c1, :])
+        def quantize_w(u):
+            codes = work.tile([P, QT], U32, name="w_codes", align_bytes=64)
+            scales = work.tile([P, QT], U8, name="w_scales", align_bytes=64)
+            w_mx[u] = (codes, scales)
+            quantize(codes[:], scales[:], w_bf[u][:])
 
         def values(u):
             cols = slice(E * (u % 2), E * (u % 2 + 1))
             nc.tensor.matmul_mx(
-                out=y_banks[u % 6][:],
+                out=y_of(u),
                 lhsT=w_mx[u][0][:].bitcast(FP8X4),
                 lhsT_scale=w_mx[u][1][:],
                 rhs=v_codes[:, cols].bitcast(FP8X4),
@@ -158,166 +163,144 @@ def tile_rows_a_silu_cap_onorm_kernel(tc, qT, kT, t, v, gn, out):
                 stop=True,
             )
 
-        def square(u):
-            squares = work.tile([P, E], F32, name="squares")
-            nc.scalar.activation(
-                out=squares[:], in_=y_banks[u % 6][:], func=ACT.Square, accum_out=sum_sq[:, u : u + 1]
-            )
-
-        def statistics(u):
-            nc.vector.bn_stats(out=stats[:, u, :], in_=y_banks[u % 6][:])
-
-        def square_means(u0, u1):
-            means = stats[:, u0:u1, 1:6:3]
-            nc.vector.scalar_tensor_tensor(
-                out=half_mean_sq[:, u0:u1, :], in0=means, scalar=0.5, in1=means, op0=ALU.mult, op1=ALU.mult
-            )
-
-        def add_spread(u0, u1):
-            nc.vector.scalar_tensor_tensor(
-                out=parts[:, u0:u1, :],
-                in0=stats[:, u0:u1, 2:6:3],
-                scalar=1.0 / E,
-                in1=half_mean_sq[:, u0:u1, :],
-                op0=ALU.mult,
-                op1=ALU.add,
-            )
-
         def root(u0, u1):
-            nc.gpsimd.tensor_tensor(out=rstd[:, u0:u1], in0=mean_sq[:, u0:u1], in1=neg_half[:, : u1 - u0], op=ALU.pow)
+            nc.gpsimd.tensor_tensor(out=rstd[:, u0:u1], in0=radicand[:, u0:u1], in1=neg_half[:, : u1 - u0], op=ALU.pow)
 
-        def inverse_root_of_parts(u0, u1):
+        def statistics(i):
+            nc.vector.bn_stats(out=stats[:, i, :], in_=y_banks[i % BANKS][:].rearrange("p u e -> p e u"))
+
+        def square_means(i):
+            means = stats[:, i, 1:6:3]
             nc.vector.scalar_tensor_tensor(
-                out=mean_sq[:, u0:u1],
-                in0=parts[:, u0:u1, 0],
-                scalar=EPS,
-                in1=parts[:, u0:u1, 1],
+                out=mean_part[:, i, :], in0=means, scalar=float(E), in1=means, op0=ALU.mult, op1=ALU.mult
+            )
+
+        def root_from_statistics(i):
+            nc.vector.scalar_tensor_tensor(
+                out=radicand[:, 2 * i : 2 * i + 2],
+                in0=stats[:, i, 2:6:3],
+                scalar=SUM_EPS,
+                in1=mean_part[:, i, :],
                 op0=ALU.add,
                 op1=ALU.add,
             )
-            root(u0, u1)
+            root(2 * i, 2 * i + 2)
 
-        def inverse_root(u0, u1):
+        def square(u):
+            squares = work.tile([P, E], F32, name="squares")
+            nc.scalar.activation(out=squares[:], in_=y_of(u), func=ACT.Square, accum_out=sum_sq[:, u : u + 1])
+
+        def root_from_sums(u0, u1):
             nc.vector.tensor_scalar(
-                out=mean_sq[:, u0:u1], in0=sum_sq[:, u0:u1], scalar1=1.0 / E, scalar2=EPS, op0=ALU.mult, op1=ALU.add
+                out=radicand[:, u0:u1], in0=sum_sq[:, u0:u1], scalar1=SUM_EPS, scalar2=None, op0=ALU.add
             )
             root(u0, u1)
 
-        def normalise(u):
-            nc.vector.scalar_tensor_tensor(
-                out=result[:, u, :],
-                in0=y_banks[u % 6][:],
-                scalar=rstd[:, u : u + 1],
-                in1=gn_sb[:],
-                op0=ALU.mult,
-                op1=ALU.mult,
-            )
+        def finish(u0, u1):
+            for u in range(u0, u1):
+                nc.vector.scalar_tensor_tensor(
+                    out=result[:, u, :],
+                    in0=y_of(u),
+                    scalar=rstd[:, u : u + 1],
+                    in1=gain[:],
+                    op0=ALU.mult,
+                    op1=ALU.mult,
+                )
+            hs, qt = divmod(u0 // 2, TILES)
+            h0, h1 = HEAD_SETS[hs]
+            heads = out_view[QT * qt : QT * (qt + 1), h0 : h1 + 1 : h1 - h0, :]
+            nc.sync.dma_start(out=heads[:, u0 % 2 : u0 % 2 + u1 - u0, :], in_=result[:, u0:u1, :])
 
-        def store(u0, u1):
-            piece = u0 // 2
-            a, qt = divmod(piece, TILES)
-            h0, h1 = HEAD_SETS[a]
-            rows = out_view[QT * qt : QT * (qt + 1), h0 : h1 + 1 : h1 - h0, :]
-            nc.sync.dma_start(out=rows[:, u0 % 2 : u0 % 2 + u1 - u0, :], in_=result[:, u0:u1, :])
-
-        load_q_mid(0, QT)
+        load_first_set(0, QT)
         for c in range(2):
-            nc.sync.dma_start(out=k_raw[c][:], in_=k_view[:, :, HALF * c : HALF * (c + 1)])
-        nc.scalar.dma_start(out=t_sb[:], in_=t.rearrange("(p j) o -> p (j o)", j=PACK))
-        load_q_mid(QT, 2 * QT)
+            nc.sync.dma_start(out=k_raw[c][:], in_=k_view[:, :, KEY_HALF * c : KEY_HALF * (c + 1)])
+        nc.scalar.dma_start(out=t_sb[:], in_=t.rearrange("(s r) o -> s (r o)", r=PACK))
+        load_first_set(QT, 2 * QT)
         nc.sync.dma_start(
-            out=v_raw[:].rearrange("p g j e -> p g (j e)"), in_=v.rearrange("g (p j) e -> p g (j e)", j=PACK)
+            out=v_raw[:].rearrange("s g r e -> s g (r e)"), in_=v.rearrange("g (s r) e -> s g (r e)", r=PACK)
         )
-        load_q_mid(2 * QT, NQ)
-        for half in range(2):
-            for g in range(2):
-                load_q_outer(g, 2 * QT * half, 2 * QT * (half + 1))
-            if half == 0:
-                nc.sync.dma_start(out=gn_sb[:], in_=gn[:, :])
+        load_first_set(2 * QT, NQ)
+        load_second_set(0, 2 * QT)
+        nc.sync.dma_start(out=gn_sb[:], in_=gn[:, :])
+        load_second_set(2 * QT, NQ)
 
         nc.gpsimd.memset(neg_half[:], -0.5)
-        nc.scalar.activation(out=warm[:], in_=neg_half[:, :2], func=ACT.Silu)
+        nc.scalar.activation(out=warm[:], in_=neg_half[:], func=ACT.Silu)
 
         copy_q(0)
+        nc.vector.tensor_copy(out=t_wide[:], in_=t_sb[:].unsqueeze(1).to_broadcast([P, QT, PACK]))
         for c in range(2):
-            copy_k(nc.scalar.copy, c, K_SPLIT, 64)
-            copy_k(nc.vector.tensor_copy, c, 0, K_SPLIT)
+            copy_k(nc.scalar.copy, c, S_VECTOR, S_HALF)
+            copy_k(nc.vector.tensor_copy, c, 0, S_VECTOR)
             if c == 0:
                 quantize_q(0)
             quantize_k(c)
         scores(0)
         scores(1)
         copy_q(1)
-        interleave(nc.vector.tensor_copy, v_bf[:, 0, :, :], v_raw[:, 0, :, :])
+        interleave(v_bf[:, 0, :, :], v_raw[:, 0, :, :])
         quantize_q(1)
-        interleave(nc.vector.tensor_copy, v_bf[:, 1, :, :], v_raw[:, 1, :, :])
+        scores(2)
+        scores(3)
+        interleave(v_bf[:, 1, :, :], v_raw[:, 1, :, :])
         copy_q(2)
         copy_q(3)
-        quantize(v_codes[:], v_scales[:], v_bf[:].rearrange("p g e j -> p (g e) j"))
+        quantize(v_codes[:], v_scales[:], v_bf[:].rearrange("s g e r -> s (g e) r"))
         quantize_q(2)
         cap(0)
         cap(1)
 
-        for i in range(7):
+        for i in range(PAIRS - 1):
             a, b = 2 * i, 2 * i + 1
-            scores(a + 2)
-            scores(b + 2)
-            if i >= 1:
-                values(a - 2)
-                values(b - 2)
+            for u in (a, b):
+                if i >= 1:
+                    values(u - 2)
+                if i + 2 < PAIRS:
+                    scores(u + 4)
             silu(a)
             silu(b)
             cap(a + 2)
             cap(b + 2)
             weigh(a)
             if i >= 2:
-                add_spread(a - 4, a - 2)
+                square_means(i - 2)
             weigh(b)
             if i >= 2:
-                inverse_root_of_parts(a - 4, a - 2)
-            quantize_w(a)
-            if 1 <= i <= 5:
-                statistics(a - 2)
-                statistics(b - 2)
-            if i >= 3:
-                normalise(a - 6)
-                normalise(b - 6)
-                store(a - 6, a - 4)
-            quantize_w(b)
-            if 1 <= i <= 5:
-                square_means(a - 2, a)
-            if i <= 4:
+                root_from_statistics(i - 2)
+            if i + 3 < PAIRS:
                 quantize_q(i + 3)
-            if i <= 3:
+            quantize_w(a)
+            if 0 <= i - 1 < FIRST_SCALAR_PAIR:
+                statistics(i - 1)
+            if i == 1:
+                nc.vector.tensor_scalar(out=gain[:], in0=gn_sb[:], scalar1=math.sqrt(E), scalar2=None, op0=ALU.mult)
+            if i >= 3:
+                finish(a - 6, a - 4)
+            quantize_w(b)
+            if i + 4 < PAIRS:
                 copy_q(i + 4)
-        values(12)
-        values(13)
-        silu(14)
-        silu(15)
-        for u in range(10, 14):
+
+        a, b = UNITS - 2, UNITS - 1
+        values(a - 2)
+        values(b - 2)
+        silu(a)
+        silu(b)
+        for u in range(2 * FIRST_SCALAR_PAIR, a):
             square(u)
-        weigh(14)
-        weigh(15)
-        normalise(8)
-        quantize_w(14)
-        values(14)
-        square(14)
-        normalise(9)
-        store(8, 10)
-        quantize_w(15)
-        values(15)
-        square(15)
-        inverse_root(10, 12)
-        inverse_root(12, 14)
-        normalise(10)
-        inverse_root(14, 15)
-        normalise(11)
-        store(10, 12)
-        inverse_root(15, 16)
-        normalise(12)
-        normalise(13)
-        store(12, 14)
-        normalise(14)
-        store(14, 15)
-        normalise(15)
-        store(15, 16)
+        weigh(a)
+        weigh(b)
+        root_from_sums(a - 4, a - 2)
+        quantize_w(a)
+        values(a)
+        square(a)
+        finish(a - 6, a - 4)
+        quantize_w(b)
+        values(b)
+        square(b)
+        root_from_sums(a - 2, a)
+        finish(a - 4, a - 2)
+        root_from_sums(a, b)
+        root_from_sums(b, UNITS)
+        finish(a - 2, a)
+        finish(a, b)
+        finish(b, UNITS)

import math
from contextlib import ExitStack

import concourse.mybir as mybir

H, KV, D, NQ, N, E = 4, 2, 256, 512, 512, 128
FLOPS = 2 * H * N * NQ * D + 2 * H * NQ * N * E

F32 = mybir.dt.float32
BF16 = mybir.dt.bfloat16
U32 = mybir.dt.uint32
U8 = mybir.dt.uint8
FP8X4 = mybir.dt.float8_e4m3fn_x4
ACT = mybir.ActivationFunctionType
ALU = mybir.AluOpType

P = 128
ROWS = 64
PACK = 4
QT = 128
TILES = NQ // QT
UNITS = H * TILES
PAIRS = UNITS // 2
BANKS = 4

HEAD_SETS = ((1, 2), (0, 3))

KEY_HALF = N // 2
S_HALF = KEY_HALF // PACK
S_VECTOR = 44

SUM_EPS = E * 1e-5 * 16.0**2

FIRST_SCALAR_PAIR = 5


def tile_rows_a_silu_cap_onorm_kernel(tc, qT, kT, t, v, gn, out):
    nc = tc.nc
    with ExitStack() as ctx:
        keep = ctx.enter_context(tc.tile_pool(name="keep", bufs=1))
        work = ctx.enter_context(tc.tile_pool(name="work", bufs=UNITS))
        psum = ctx.enter_context(tc.psum_pool(name="psum", bufs=1))
        ctx.enter_context(tc.manual_schedule())

        k_raw = [keep.tile([P, PACK, KEY_HALF], F32, name="k_raw%d" % c) for c in range(2)]
        q_raw = [keep.tile([P, PACK, NQ], F32, name="q_raw%d" % hs) for hs in range(2)]
        v_raw = keep.tile([P, KV, PACK, E], F32)
        t_sb = keep.tile([P, PACK], F32)
        t_wide = keep.tile([P, QT, PACK], F32)
        gn_sb = keep.tile([P, E], F32)
        k_bf = keep.tile([P, PACK, P, PACK], BF16, align_bytes=64)
        q_bf = keep.tile([P, 2, NQ, PACK], BF16, align_bytes=64)
        v_bf = keep.tile([P, KV, E, PACK], BF16, align_bytes=64)
        k_codes = keep.tile([P, N], U32, align_bytes=64)
        k_scales = keep.tile([P, N], U8, align_bytes=64)
        q_codes = keep.tile([P, 2, NQ], U32, align_bytes=64)
        q_scales = keep.tile([P, 2, NQ], U8, align_bytes=64)
        v_codes = keep.tile([P, KV * E], U32, align_bytes=64)
        v_scales = keep.tile([P, KV * E], U8, align_bytes=64)
        neg_half = keep.tile([P, 2], F32)
        warm = keep.tile([P, 2], F32)
        stats = keep.tile([P, PAIRS, 6], F32)
        mean_part = keep.tile([P, PAIRS, 2], F32)
        sum_sq = keep.tile([P, UNITS], F32)
        radicand = keep.tile([P, UNITS], F32)
        rstd = keep.tile([P, UNITS], F32)
        gain = keep.tile([P, E], F32)
        result = keep.tile([P, UNITS, E], F32)
        score_banks = [psum.tile([P, PACK, QT], F32, name="scores%d" % n) for n in range(BANKS)]
        y_banks = [psum.tile([P, 2, E], F32, name="y%d" % n) for n in range(BANKS)]

        capped, p_tiles, w_bf, w_mx = {}, {}, {}, {}

        k_view = kT.rearrange("g (p j) n -> (g p) j n", j=PACK)
        q_first = qT[HEAD_SETS[0][0] : HEAD_SETS[0][1] + 1].rearrange("g (p j) n -> (g p) j n", j=PACK)
        out_view = out.rearrange("h q e -> q h e")

        def y_of(u):
            if u == UNITS - 1:
                return y_banks[0][:, 0, :]
            return y_banks[u // 2 % BANKS][:, u % 2, :]

        def load_first_set(c0, c1):
            nc.sync.dma_start(out=q_raw[0][:, :, c0:c1], in_=q_first[:, :, c0:c1])

        def load_second_set(c0, c1):
            for g in range(KV):
                head = qT[HEAD_SETS[1][g]].rearrange("(p j) n -> p j n", j=PACK)
                nc.sync.dma_start(out=q_raw[1][ROWS * g : ROWS * (g + 1), :, c0:c1], in_=head[:, :, c0:c1])

        def interleave(dst, src):
            nc.vector.tensor_copy(
                out=dst.rearrange("p (c x) j -> p c j x", x=4), in_=src.rearrange("p j (c x) -> p c j x", x=4)
            )

        def quantize(codes, scales, src):
            nc.vector.quantize_mx(out=codes.bitcast(FP8X4), scales=scales, in_=src.rearrange("p c j -> p (c j)"))

        def copy_k(copy, c, s0, s1):
            dst = k_bf[:, :, S_HALF * c + s0 : S_HALF * c + s1, :].rearrange("p r s j -> p s j r")
            copy(out=dst, in_=k_raw[c][:].rearrange("p j (s r) -> p s j r", r=PACK)[:, s0:s1, :, :])

        def quantize_k(c):
            for r in range(PACK):
                cols = slice(P * r + S_HALF * c, P * r + S_HALF * (c + 1))
                quantize(k_codes[:, cols], k_scales[:, cols], k_bf[:, r, S_HALF * c : S_HALF * (c + 1), :])

        def copy_q(i):
            hs, qt = divmod(i, TILES)
            cols = slice(QT * qt, QT * (qt + 1))
            interleave(q_bf[:, hs, cols, :], q_raw[hs][:, :, cols])

        def quantize_q(i):
            hs, qt = divmod(i, TILES)
            cols = slice(QT * qt, QT * (qt + 1))
            quantize(q_codes[:, hs, cols], q_scales[:, hs, cols], q_bf[:, hs, cols, :])

        def scores(u):
            hs, qt = divmod(u // 2, TILES)
            rows = slice(ROWS * (u % 2), ROWS * (u % 2 + 1))
            cols = slice(QT * qt, QT * (qt + 1))
            for r in range(PACK):
                tokens = slice(P * r, P * (r + 1))
                nc.tensor.matmul_mx(
                    out=score_banks[u % BANKS][:, r, :],
                    lhsT=k_codes[rows, tokens].bitcast(FP8X4),
                    lhsT_scale=k_scales[rows, tokens],
                    rhs=q_codes[rows, hs, cols].bitcast(FP8X4),
                    rhs_scale=q_scales[rows, hs, cols],
                    start=True,
                    stop=True,
                )

        def cap(u):
            capped[u] = work.tile([P, QT, PACK], F32, name="capped")
            nc.scalar.activation(
                out=capped[u][:], in_=score_banks[u % BANKS][:].rearrange("p r q -> p q r"), func=ACT.Tanh, scale=0.5
            )

        def silu(u):
            p_tiles[u] = work.tile([P, QT, PACK], F32, name="p")
            nc.scalar.activation(out=p_tiles[u][:], in_=capped[u][:], func=ACT.Silu, scale=2.0)

        def weigh(u):
            w_bf[u] = work.tile([P, QT, PACK], BF16, name="w_bf", align_bytes=64)
            nc.vector.tensor_tensor(out=w_bf[u][:], in0=p_tiles[u][:], in1=t_wide[:], op=ALU.mult)

        def quantize_w(u):
            codes = work.tile([P, QT], U32, name="w_codes", align_bytes=64)
            scales = work.tile([P, QT], U8, name="w_scales", align_bytes=64)
            w_mx[u] = (codes, scales)
            quantize(codes[:], scales[:], w_bf[u][:])

        def values(u):
            cols = slice(E * (u % 2), E * (u % 2 + 1))
            nc.tensor.matmul_mx(
                out=y_of(u),
                lhsT=w_mx[u][0][:].bitcast(FP8X4),
                lhsT_scale=w_mx[u][1][:],
                rhs=v_codes[:, cols].bitcast(FP8X4),
                rhs_scale=v_scales[:, cols],
                start=True,
                stop=True,
            )

        def root(u0, u1):
            nc.gpsimd.tensor_tensor(out=rstd[:, u0:u1], in0=radicand[:, u0:u1], in1=neg_half[:, : u1 - u0], op=ALU.pow)

        def statistics(i):
            nc.vector.bn_stats(out=stats[:, i, :], in_=y_banks[i % BANKS][:].rearrange("p u e -> p e u"))

        def square_means(i):
            means = stats[:, i, 1:6:3]
            nc.vector.scalar_tensor_tensor(
                out=mean_part[:, i, :], in0=means, scalar=float(E), in1=means, op0=ALU.mult, op1=ALU.mult
            )

        def root_from_statistics(i):
            nc.vector.scalar_tensor_tensor(
                out=radicand[:, 2 * i : 2 * i + 2],
                in0=stats[:, i, 2:6:3],
                scalar=SUM_EPS,
                in1=mean_part[:, i, :],
                op0=ALU.add,
                op1=ALU.add,
            )
            root(2 * i, 2 * i + 2)

        def square(u):
            squares = work.tile([P, E], F32, name="squares")
            nc.scalar.activation(out=squares[:], in_=y_of(u), func=ACT.Square, accum_out=sum_sq[:, u : u + 1])

        def root_from_sums(u0, u1):
            nc.vector.tensor_scalar(
                out=radicand[:, u0:u1], in0=sum_sq[:, u0:u1], scalar1=SUM_EPS, scalar2=None, op0=ALU.add
            )
            root(u0, u1)

        def finish(u0, u1):
            for u in range(u0, u1):
                nc.vector.scalar_tensor_tensor(
                    out=result[:, u, :],
                    in0=y_of(u),
                    scalar=rstd[:, u : u + 1],
                    in1=gain[:],
                    op0=ALU.mult,
                    op1=ALU.mult,
                )
            hs, qt = divmod(u0 // 2, TILES)
            h0, h1 = HEAD_SETS[hs]
            heads = out_view[QT * qt : QT * (qt + 1), h0 : h1 + 1 : h1 - h0, :]
            nc.sync.dma_start(out=heads[:, u0 % 2 : u0 % 2 + u1 - u0, :], in_=result[:, u0:u1, :])

        load_first_set(0, QT)
        for c in range(2):
            nc.sync.dma_start(out=k_raw[c][:], in_=k_view[:, :, KEY_HALF * c : KEY_HALF * (c + 1)])
        nc.scalar.dma_start(out=t_sb[:], in_=t.rearrange("(s r) o -> s (r o)", r=PACK))
        load_first_set(QT, 2 * QT)
        nc.sync.dma_start(
            out=v_raw[:].rearrange("s g r e -> s g (r e)"), in_=v.rearrange("g (s r) e -> s g (r e)", r=PACK)
        )
        load_first_set(2 * QT, NQ)
        load_second_set(0, 2 * QT)
        nc.sync.dma_start(out=gn_sb[:], in_=gn[:, :])
        load_second_set(2 * QT, NQ)

        nc.gpsimd.memset(neg_half[:], -0.5)
        nc.scalar.activation(out=warm[:], in_=neg_half[:], func=ACT.Silu)

        copy_q(0)
        nc.vector.tensor_copy(out=t_wide[:], in_=t_sb[:].unsqueeze(1).to_broadcast([P, QT, PACK]))
        for c in range(2):
            copy_k(nc.scalar.copy, c, S_VECTOR, S_HALF)
            copy_k(nc.vector.tensor_copy, c, 0, S_VECTOR)
            if c == 0:
                quantize_q(0)
            quantize_k(c)
        scores(0)
        scores(1)
        copy_q(1)
        interleave(v_bf[:, 0, :, :], v_raw[:, 0, :, :])
        quantize_q(1)
        scores(2)
        scores(3)
        interleave(v_bf[:, 1, :, :], v_raw[:, 1, :, :])
        copy_q(2)
        copy_q(3)
        quantize(v_codes[:], v_scales[:], v_bf[:].rearrange("s g e r -> s (g e) r"))
        quantize_q(2)
        cap(0)
        cap(1)

        for i in range(PAIRS - 1):
            a, b = 2 * i, 2 * i + 1
            for u in (a, b):
                if i >= 1:
                    values(u - 2)
                if i + 2 < PAIRS:
                    scores(u + 4)
            silu(a)
            silu(b)
            cap(a + 2)
            cap(b + 2)
            weigh(a)
            if i >= 2:
                square_means(i - 2)
            weigh(b)
            if i >= 2:
                root_from_statistics(i - 2)
            if i + 3 < PAIRS:
                quantize_q(i + 3)
            quantize_w(a)
            if 0 <= i - 1 < FIRST_SCALAR_PAIR:
                statistics(i - 1)
            if i == 1:
                nc.vector.tensor_scalar(out=gain[:], in0=gn_sb[:], scalar1=math.sqrt(E), scalar2=None, op0=ALU.mult)
            if i >= 3:
                finish(a - 6, a - 4)
            quantize_w(b)
            if i + 4 < PAIRS:
                copy_q(i + 4)

        a, b = UNITS - 2, UNITS - 1
        values(a - 2)
        values(b - 2)
        silu(a)
        silu(b)
        for u in range(2 * FIRST_SCALAR_PAIR, a):
            square(u)
        weigh(a)
        weigh(b)
        root_from_sums(a - 4, a - 2)
        quantize_w(a)
        values(a)
        square(a)
        finish(a - 6, a - 4)
        quantize_w(b)
        values(b)
        square(b)
        root_from_sums(a - 2, a)
        finish(a - 4, a - 2)
        root_from_sums(a, b)
        root_from_sums(b, UNITS)
        finish(a - 2, a)
        finish(a, b)
        finish(b, UNITS)
